import numpy as np
import ml_dtypes


def mxq(x, axis, fmt="e4m3"):
    dtype, down = {"e4m3": (ml_dtypes.float8_e4m3fn, 7), "e5m2": (ml_dtypes.float8_e5m2, 14)}[fmt]
    v = np.moveaxis(np.asarray(x, np.float32).astype(ml_dtypes.bfloat16).astype(np.float64), axis, -1)
    blocks = v.reshape(v.shape[:-1] + (-1, 32))
    amax = np.abs(blocks).max(-1, keepdims=True)
    byte = np.maximum(np.where(amax > 0, np.frexp(amax)[1] - 1 + 127, 0) - down, 1)
    scale = np.exp2(byte - 127.0)
    codes = (blocks / scale).astype(np.float32).astype(dtype).astype(np.float64)
    return np.moveaxis((codes * scale).reshape(v.shape), -1, axis)


WIDE = False


def mx_kscale(k):
    if not WIDE:
        return np.ones(k)
    levels = np.array([10, -10, 5, -5, 0])
    if k % 512:
        return np.exp2(np.random.permutation(np.resize(levels, k // 32))).repeat(32)
    a = np.empty((k // 512, 16))
    for p in range(k // 512):
        a[p, :8] = np.random.permutation(np.resize(levels, 8))
        for g in range(8):
            far = levels[np.abs(levels - a[p, g]) >= 10]
            a[p, g + 8] = far[np.random.randint(len(far))]
    return np.exp2(a.ravel()).repeat(32)


BF16 = ml_dtypes.bfloat16


def bf(x):
    return np.asarray(x, np.float32).astype(BF16)


def f64(x):
    return np.asarray(x).astype(np.float64)

def planes(Y):
    n, m = Y.shape
    b = f64(bf(Y)).reshape(n // 32, 32, m)
    amax = np.abs(b).max(1)
    byte = np.clip(np.where(amax > 0, np.frexp(amax)[1] - 1 + 127 - 7, 1), 1, 254)
    codes = (b * np.exp2(127.0 - byte)[:, None, :]).reshape(n, m).astype(np.float32).astype(ml_dtypes.float8_e4m3fn).view(np.uint8)
    words = codes.reshape(n // 512, 128, 4, m).transpose(0, 1, 3, 2)
    return np.ascontiguousarray(words), np.ascontiguousarray(byte.astype(np.uint8).reshape(n // 512, 16, m))


B, N, M, P = 512, 1024, 1024, 1024


def setup_inputs():
    s, u = mx_kscale(N), mx_kscale(M)
    t = np.random.standard_normal((B, N)) * s[None, :]
    i1 = np.random.uniform(0.0, 2.0, (M, N)) / np.sqrt(N) / s[None, :]
    r = np.random.uniform(0.5, 2.5, M)
    q = (1.0 + 0.1 * np.random.standard_normal(M)) * u
    i2 = np.random.standard_normal((M, P)) / u[:, None]
    return {"t": bf(t), "i1": bf(i1), "r": bf(r), "q": bf(q), "i2": bf(i2)}


def bucket_signals(t, i1):
    return mxq(t, 1, "e4m3") @ mxq(i1, 1, "e4m3").T


def differential_signal(s, r):
    sbar = np.mean(s, axis=1)
    rbar = np.mean(r)
    return s - (sbar / rbar)[:, None] * r[None, :]


def core(t, i1, r, q, i2):
    shots = i2.shape[0]
    s = bucket_signals(f64(t), f64(i1))
    d = differential_signal(s, f64(r))
    e = d * f64(q)[None, :]
    return (mxq(e, 1, "e4m3") @ mxq(f64(i2), 0, "e4m3")) / np.sqrt(shots)


def reference(t, i1, r, q, i2):
    R_out = core(t, i1, r, q, i2)
    words, scales = planes(R_out)
    return R_out, words, scales

@@ -1,0 +1,512 @@
+from contextlib import ExitStack
+
+import concourse.mybir as mybir
+from concourse.masks import make_identity
+
+F32 = mybir.dt.float32
+BF16 = mybir.dt.bfloat16
+U32 = mybir.dt.uint32
+I32 = mybir.dt.int32
+U8 = mybir.dt.uint8
+FP8X4 = mybir.dt.float8_e4m3fn_x4
+ADD = mybir.AluOpType.add
+MULT = mybir.AluOpType.mult
+COPY = mybir.ActivationFunctionType.Copy
+
+B, N, M, C = 512, 1024, 1024, 1024
+FLOPS = 2 * B * N * M + 2 * B * M * C
+P = 128
+BLOCKS = ((0, 2), (2, 2))
+
+
+def tile_weighteddifferentialghostimage_x1_kernel(tc, t, i1, r, q, i2, out_0, out_1, out_2):
+    nc = tc.nc
+    with ExitStack() as ctx:
+        keep = ctx.enter_context(tc.tile_pool(name="keep", bufs=1))
+        stage = ctx.enter_context(tc.tile_pool(name="stage", bufs=3))
+        psum_tr = ctx.enter_context(tc.psum_pool(name="psum_tr", bufs=3))
+        psum_s = ctx.enter_context(tc.psum_pool(name="psum_s", bufs=4))
+        psum_m = ctx.enter_context(tc.psum_pool(name="psum_m", bufs=1))
+        ctx.enter_context(tc.manual_schedule())
+
+        t_v = t.rearrange("(p s) n -> p s n", s=4)
+        i1_v = i1.rearrange("(g p s) n -> g p s n", g=2, s=4)
+        i2_v = i2.rearrange("(g p j) c -> g p j c", g=2, j=4)
+        q_b = keep.tile([P, 2, 4], BF16, name="q_b")
+        r_b = keep.tile([P, 2, 4], BF16, name="r_b")
+        nc.scalar.dma_start(out=r_b[:], in_=r.rearrange("(g p s) -> p g s", g=2, s=4))
+        nc.scalar.dma_start(out=q_b[:], in_=q.rearrange("(g p s) -> p g s", g=2, s=4))
+
+        t_sb = [None] * 4
+        i1_sb = [None] * 4
+        i2_sb = [None] * 4
+
+        def load_t(s):
+            t_sb[s] = keep.tile([P, N], BF16, name="t_sb%d" % s, align_bytes=64)
+            nc.sync.dma_start(out=t_sb[s][:], in_=t_v[:, s, :])
+
+        def load_i1(a):
+            i1_sb[a] = keep.tile([P, 2, N], BF16, name="i1_sb%d" % a, align_bytes=64)
+            nc.sync.dma_start(out=i1_sb[a][:], in_=i1_v[a // 2][:, 2 * (a % 2) : 2 * (a % 2) + 2, :])
+
+        def load_i2(a):
+            i2_sb[a] = keep.tile([P, 4, 512], BF16, name="i2_sb%d" % a, align_bytes=64)
+            nc.sync.dma_start(out=i2_sb[a][:], in_=i2_v[a // 2][:, :, 512 * (a % 2) : 512 * (a % 2) + 512])
+
+
+        ident = keep.tile([P, P], F32, name="ident")
+        make_identity(nc, ident[:])
+        ones = keep.tile([P, P], F32, name="ones")
+        nc.gpsimd.memset(ones[:], 1.0)
+
+        def copy(engine, dst, src):
+            if engine == "A":
+                nc.scalar.copy(out=dst, in_=src)
+            else:
+                nc.vector.tensor_copy(out=dst, in_=src)
+
+        def turn(rows):
+            bank = psum_tr.tile([P, 4, P], F32, name="bank_tr", tag="tr")
+            words = rows.bitcast(F32)
+            for g in range(2):
+                for u in range(2):
+                    nc.tensor.transpose(bank[:, 2 * g + u, :], words[:, 256 * g + u : 256 * (g + 1) : 2], ident[:])
+            return bank
+
+        def evac(engine, dst, bank):
+            src = bank[:].rearrange("p (g u) r -> p g r u", g=2)
+            if engine == "A":
+                nc.scalar.copy(out=dst, in_=src)
+            else:
+                nc.vector.tensor_copy(out=dst, in_=src)
+
+        def quant(src, codes, scales):
+            nc.vector.quantize_mx(out=codes.bitcast(FP8X4), scales=scales, in_=src)
+
+        t_codes = {}
+        t_scales = {}
+        t_grp = {}
+        t_bank = {}
+
+        def width(h):
+            return P * BLOCKS[h][1]
+
+        def turn_t(s):
+            t_bank[s] = turn(t_sb[s][:])
+
+        def evac_t(h, engines):
+            s0, ns = BLOCKS[h]
+            t_grp[h] = stage.tile([P, 2 * ns * P * 4], BF16, name="t_grp", tag="t_grp", align_bytes=64)
+            dst = t_grp[h][:].bitcast(F32).rearrange("p (g s r u) -> p g s r u", g=2, s=ns, u=2)
+            for s in range(ns):
+                evac(engines[s], dst[:, :, s], t_bank[s0 + s])
+
+        def evac_t1(s, engine):
+            h = [k for k in range(len(BLOCKS)) if BLOCKS[k][0] <= s < BLOCKS[k][0] + BLOCKS[k][1]][0]
+            s0, ns = BLOCKS[h]
+            dst = t_grp[h][:].bitcast(F32).rearrange("p (g s r u) -> p g s r u", g=2, s=ns, u=2)
+            evac(engine, dst[:, :, s - s0], t_bank[s])
+
+        def quant_t(h):
+            t_codes[h] = keep.tile([P, 2, width(h)], U32, name="t_codes%d" % h, align_bytes=64)
+            t_scales[h] = keep.tile([P, 2, width(h)], U8, name="t_scales%d" % h, align_bytes=64)
+            quant(t_grp[h][:], t_codes[h][:].rearrange("p g b -> p (g b)"), t_scales[h][:].rearrange("p g b -> p (g b)"))
+
+        i1_codes = [None] * 4
+        i1_scales = [None] * 4
+        i1_grp = [None] * 4
+        i1_bank = {}
+
+        def turn_i1(a):
+            for s in range(2):
+                i1_bank[2 * a + s] = turn(i1_sb[a][:, s, :])
+
+        def evac_i1(a, engines):
+            i1_grp[a] = stage.tile([P, 2 * 1024], BF16, name="i1_grp", tag="i1_grp", align_bytes=64)
+            dst = i1_grp[a][:].bitcast(F32).rearrange("p (s g r u) -> p s g r u", s=2, g=2, u=2)
+            for s in range(2):
+                evac(engines[s], dst[:, s], i1_bank[2 * a + s])
+
+        def turn_i1s(j):
+            i1_bank[j] = turn(i1_sb[j // 2][:, j % 2, :])
+
+        def evac_i1s(j, engine):
+            a = j // 2
+            dst = i1_grp[a][:].bitcast(F32).rearrange("p (s g r u) -> p s g r u", s=2, g=2, u=2)
+            evac(engine, dst[:, j % 2], i1_bank[j])
+
+        def quant_i1(a):
+            i1_codes[a] = keep.tile([P, 2, 2, P], U32, name="i1_codes%d" % a, align_bytes=64)
+            i1_scales[a] = keep.tile([P, 2, 2, P], U8, name="i1_scales%d" % a, align_bytes=64)
+            quant(i1_grp[a][:], i1_codes[a][:].rearrange("p s g r -> p (s g r)"), i1_scales[a][:].rearrange("p s g r -> p (s g r)"))
+
+        i2_codes = keep.tile([P, 2, C], U32, name="i2_codes", align_bytes=64)
+        i2_scales = keep.tile([P, 2, C], U8, name="i2_scales", align_bytes=64)
+        i2_grp = [None] * 4
+
+        def mix_i2(a, engine):
+            i2_grp[a] = stage.tile([P, 512, 4], BF16, name="i2_grp", tag="i2_grp", align_bytes=64)
+            src = i2_sb[a][:].rearrange("p j c -> p c j")
+            if engine == "A":
+                nc.scalar.copy(out=i2_grp[a][:], in_=src)
+            else:
+                nc.vector.tensor_copy(out=i2_grp[a][:], in_=src)
+
+        def mix_i2h(a, half, engine):
+            cols = slice(256 * half, 256 * half + 256)
+            copy(engine, i2_grp[a][:, cols, :], i2_sb[a][:, :, cols].rearrange("p j c -> p c j"))
+
+        def quant_i2(a):
+            cols = slice(512 * (a % 2), 512 * (a % 2) + 512)
+            quant(i2_grp[a][:].rearrange("p c j -> p (c j)"), i2_codes[:, a // 2, cols], i2_scales[:, a // 2, cols])
+
+        s_bank = {}
+        mean_bank = {}
+
+        def mx1(out, j, h, g, start, stop):
+            nc.tensor.matmul_mx(
+                out=out,
+                lhsT=i1_codes[j // 2][:, j % 2, g, :].bitcast(FP8X4),
+                lhsT_scale=i1_scales[j // 2][:, j % 2, g, :],
+                rhs=t_codes[h][:, g, :].bitcast(FP8X4),
+                rhs_scale=t_scales[h][:, g, :],
+                start=start,
+                stop=stop,
+            )
+
+        def s_of(h, j):
+            per = 4 // BLOCKS[h][1]
+            return s_bank[(h, j // per)][:, width(h) * (j % per) : width(h) * (j % per + 1)]
+
+        def mx_s(h, j):
+            per = 4 // BLOCKS[h][1]
+            if j % per == 0:
+                s_bank[(h, j // per)] = psum_s.tile([P, 512], F32, name="bank_s", tag="s")
+            for g in range(2):
+                mx1(s_of(h, j), j, h, g, g == 0, g == 1)
+
+        def mx_mean(h, j):
+            if j == 0:
+                mean_bank[h] = psum_m.tile([P, width(h)], F32, name="bank_m", tag="m")
+            for g in range(2):
+                mx1(mean_bank[h][:], j, h, g, j == 0 and g == 0, j == 7 and g == 1)
+
+        total = {}
+
+        part = {}
+
+        def part_sum(h, engine):
+            part[h] = stage.tile([P, width(h)], F32, name="part", tag="part")
+            copy(engine, part[h][:], mean_bank[h][:])
+
+        def acc_v(h, j):
+            if j == 0:
+                part[h] = stage.tile([P, width(h)], F32, name="part", tag="part")
+                nc.vector.tensor_copy(out=part[h][:], in_=s_of(h, 0))
+            else:
+                nc.vector.tensor_tensor(out=part[h][:], in0=part[h][:], in1=s_of(h, j), op=ADD)
+
+        def sum_mm(h):
+            total[h] = psum_tr.tile([P, 4, P], F32, name="bank_tr", tag="tr")
+            nc.tensor.matmul(total[h][:].rearrange("p a b -> p (a b)")[:, :width(h)], lhsT=ones[:], rhs=part[h][:], start=True, stop=True)
+
+        total_sb = {}
+
+        def sum_out(h, engine):
+            total_sb[h] = stage.tile([P, width(h)], F32, name="total_sb", tag="total_sb")
+            copy(engine, total_sb[h][:], total[h][:].rearrange("p a b -> p (a b)")[:, : width(h)])
+
+        q_f = keep.tile([P, 8], F32, name="q_f")
+        r_f = keep.tile([P, 8], F32, name="r_f")
+        r_neg = keep.tile([P, 8], F32, name="r_neg")
+        w_neg = keep.tile([P, 8], F32, name="w_neg")
+        r_bank = []
+
+        def consts_a(engine):
+            copy(engine, q_f[:], q_b[:].rearrange("p g s -> p (g s)"))
+            copy(engine, r_f[:], r_b[:].rearrange("p g s -> p (g s)"))
+
+        def consts_mm():
+            r_bank.append(psum_tr.tile([P, 4, P], F32, name="bank_tr", tag="tr"))
+            nc.tensor.matmul(r_bank[0][:, 0, :8], lhsT=ones[:], rhs=r_f[:], start=True, stop=True)
+
+        def consts_b():
+            r_sum = keep.tile([P, 1], F32, name="r_sum")
+            r_inv = keep.tile([P, 1], F32, name="r_inv")
+            nc.vector.reduce_sum(out=r_sum[:], in_=r_bank[0][:, 0, :8], axis=mybir.AxisListType.X)
+            nc.vector.reciprocal(out=r_inv[:], in_=r_sum[:])
+            nc.vector.tensor_scalar(out=r_neg[:], in0=r_f[:], scalar1=r_inv[:], scalar2=-1.0, op0=MULT, op1=MULT)
+            nc.vector.tensor_mul(out=w_neg[:], in0=r_neg[:], in1=q_f[:])
+
+        e_grp = {}
+        e_codes = {}
+        e_scales = {}
+        d_sb = {}
+        z_sb = {}
+
+        def e_u1(h, g):
+            for k in range(4):
+                j = 4 * g + k
+                nc.vector.scalar_tensor_tensor(
+                    out=d_sb[(h, g)][:, k, :], in0=total_sb[h][:], scalar=r_neg[:, j : j + 1], in1=s_of(h, j), op0=MULT, op1=ADD
+                )
+
+        def e_out(h, g):
+            return e_grp[(h, g)][:].rearrange("p (b k) -> p b k", k=4)
+
+        def e_u2(h, g):
+            nc.vector.tensor_tensor(
+                out=e_out(h, g),
+                in0=d_sb[(h, g)][:].rearrange("p k b -> p b k"),
+                in1=q_f[:, 4 * g : 4 * g + 4].unsqueeze(1).to_broadcast([P, width(h), 4]),
+                op=MULT,
+            )
+
+        def e_x(h, g, engine):
+            for k in range(4):
+                j = 4 * g + k
+                if engine == "A":
+                    nc.scalar.activation(out=d_sb[(h, g)][:, k, :], in_=s_of(h, j), func=COPY, scale=q_f[:, j : j + 1])
+                else:
+                    nc.vector.tensor_scalar_mul(d_sb[(h, g)][:, k, :], s_of(h, j), q_f[:, j : j + 1])
+
+        def e_z(h, g, engine):
+            for k in range(4):
+                j = 4 * g + k
+                if engine == "A":
+                    nc.scalar.activation(out=z_sb[(h, g)][:, k, :], in_=total_sb[h][:], func=COPY, scale=w_neg[:, j : j + 1])
+                else:
+                    nc.vector.tensor_scalar_mul(z_sb[(h, g)][:, k, :], total_sb[h][:], w_neg[:, j : j + 1])
+
+        def e_t3(h, g):
+            nc.vector.tensor_tensor(
+                out=e_out(h, g),
+                in0=d_sb[(h, g)][:].rearrange("p k b -> p b k"),
+                in1=z_sb[(h, g)][:].rearrange("p k b -> p b k"),
+                op=ADD,
+            )
+
+        def quant_e(h, g):
+            quant(e_grp[(h, g)][:], e_codes[h][:, g, :], e_scales[h][:, g, :])
+
+        y_sb = keep.tile([P, 4, C], F32, name="y_sb", align_bytes=64)
+        y_bank = {}
+
+        def mx_y(h, s, c):
+            y_bank[(h, s, c)] = psum_tr.tile([P, 4, P], F32, name="bank_tr", tag="tr")
+            cols = slice(512 * c, 512 * c + 512)
+            rows = slice(P * s, P * s + P)
+            for g in range(2):
+                nc.tensor.matmul_mx(
+                    out=y_bank[(h, s, c)][:].rearrange("p a b -> p (a b)"),
+                    lhsT=e_codes[h][:, g, rows].bitcast(FP8X4),
+                    lhsT_scale=e_scales[h][:, g, rows],
+                    rhs=i2_codes[:, g, cols].bitcast(FP8X4),
+                    rhs_scale=i2_scales[:, g, cols],
+                    start=g == 0,
+                    stop=g == 1,
+                )
+
+        def y_evac(h, s, c, engine):
+            src = y_bank[(h, s, c)][:].rearrange("p a b -> p (a b)")
+            dst = y_sb[:, BLOCKS[h][0] + s, 512 * c : 512 * c + 512]
+            if engine == "A":
+                nc.scalar.mul(dst, src, 1.0 / 32.0)
+            else:
+                nc.vector.tensor_scalar_mul(dst, src, 1.0 / 32.0)
+
+        out_v = out_0.rearrange("(p s) c -> p s c", s=4)
+
+        def y_store(s):
+            nc.sync.dma_start(out=out_v[:, s, :], in_=y_sb[:, s, :])
+
+        def y_store_half(s, c):
+            cols = slice(512 * c, 512 * c + 512)
+            nc.sync.dma_start(out=out_v[:, s, cols], in_=y_sb[:, s, cols])
+
+        y_grp = [None] * 4
+        y_codes = keep.tile([P, C], U32, name="y_codes", align_bytes=64)
+        y_scales = keep.tile([P, C], U8, name="y_scales", align_bytes=64)
+
+        def y_mix(c, engine):
+            src = y_sb[:, :, 256 * c : 256 * c + 256].rearrange("p s c -> p c s")
+            if engine == "A":
+                nc.scalar.copy(out=y_grp[c][:], in_=src)
+            else:
+                nc.vector.tensor_copy(out=y_grp[c][:], in_=src)
+
+        def y_quant(c):
+            cols = slice(256 * c, 256 * c + 256)
+            quant(y_grp[c][:].rearrange("p c s -> p (c s)"), y_codes[:, cols], y_scales[:, cols])
+
+        words_v = out_1[0].rearrange("p m s -> p (m s)").bitcast(I32)
+
+        def words_store(c):
+            cols = slice(512 * c, 512 * c + 512)
+            nc.sync.dma_start(out=words_v[:, cols], in_=y_codes[:, cols].bitcast(I32))
+
+        def scales_store():
+            dst = out_2[0].bitcast(I32)
+            for k in range(4):
+                eng = nc.scalar if k % 2 == 0 else nc.sync
+                eng.dma_start(out=dst[4 * k : 4 * k + 4, :], in_=y_scales[32 * k : 32 * k + 4, :].bitcast(I32))
+
+        for h in range(len(BLOCKS)):
+            t_grp[h] = keep.tile([P, 2 * width(h) * 4], BF16, name="t_grp%d" % h, align_bytes=64)
+            e_codes[h] = keep.tile([P, 2, width(h)], U32, name="e_codes%d" % h, align_bytes=64)
+            e_scales[h] = keep.tile([P, 2, width(h)], U8, name="e_scales%d" % h, align_bytes=64)
+            for g in range(2):
+                d_sb[(h, g)] = keep.tile([P, 4, width(h)], F32, name="d_sb%d_%d" % (h, g), align_bytes=64)
+                z_sb[(h, g)] = keep.tile([P, 4, width(h)], F32, name="z_sb%d_%d" % (h, g), align_bytes=64)
+                e_grp[(h, g)] = keep.tile([P, width(h) * 4], BF16, name="e_grp%d_%d" % (h, g), align_bytes=64)
+        for a in range(4):
+            i1_grp[a] = keep.tile([P, 2 * 1024], BF16, name="i1_grp%d" % a, align_bytes=64)
+            i2_grp[a] = keep.tile([P, 512, 4], BF16, name="i2_grp%d" % a, align_bytes=64)
+            y_grp[a] = keep.tile([P, 256, 4], BF16, name="y_grp%d" % a, align_bytes=64)
+
+        load_t(0)
+        load_t(1)
+        load_i1(0)
+        load_i1(1)
+        load_i2(0)
+        load_i1(2)
+        load_i2(1)
+        load_i1(3)
+        load_t(2)
+        load_t(3)
+        load_i2(2)
+        load_i2(3)
+        consts_a("V")
+        consts_mm()
+        turn_t(0)
+        consts_b()
+        turn_t(1)
+        evac_t1(0, "A")
+        turn_i1s(0)
+        evac_t1(1, "A")
+        turn_i1s(1)
+        evac_i1s(0, "V")
+        turn_i1s(2)
+        evac_i1s(1, "A")
+        quant_t(0)
+        turn_i1s(3)
+        evac_i1s(2, "A")
+        quant_i1(0)
+        evac_i1s(3, "A")
+        mx_mean(0, 0)
+        mx_s(0, 0)
+        mix_i2h(0, 1, "A")
+        quant_i1(1)
+        mx_mean(0, 1)
+        mx_s(0, 1)
+        mix_i2h(0, 0, "V")
+        turn_i1s(4)
+        turn_i1s(5)
+        mix_i2h(1, 0, "A")
+        evac_i1s(4, "V")
+        mx_mean(0, 2)
+        evac_i1s(5, "V")
+        mx_s(0, 2)
+        mx_mean(0, 3)
+        mix_i2h(1, 1, "A")
+        quant_i1(2)
+        mx_s(0, 3)
+        turn_i1s(6)
+        quant_i2(0)
+        turn_i1s(7)
+        evac_i1s(6, "A")
+        quant_i2(1)
+        mx_mean(0, 4)
+        evac_i1s(7, "A")
+        mx_s(0, 4)
+        mix_i2h(2, 1, "V")
+        mx_mean(0, 5)
+        mx_s(0, 5)
+        quant_i1(3)
+        turn_t(2)
+        mix_i2h(3, 1, "A")
+        mix_i2h(2, 0, "V")
+        turn_t(3)
+        mx_mean(0, 6)
+        mix_i2h(3, 0, "V")
+        mx_s(0, 6)
+        evac_t1(2, "A")
+        mx_mean(0, 7)
+        evac_t1(3, "V")
+        mx_s(0, 7)
+        part_sum(0, "A")
+        quant_i2(3)
+        sum_mm(0)
+        quant_t(1)
+        sum_out(0, "A")
+        quant_i2(2)
+        e_x(0, 1, "A")
+        mx_mean(1, 0)
+        mx_mean(1, 1)
+        e_z(0, 1, "V")
+        mx_mean(1, 2)
+        mx_mean(1, 3)
+        mx_mean(1, 4)
+        e_z(0, 0, "V")
+        e_x(0, 0, "A")
+        mx_mean(1, 5)
+        mx_mean(1, 6)
+        e_t3(0, 1)
+        mx_mean(1, 7)
+        mx_s(1, 0)
+        mx_s(1, 1)
+        mx_s(1, 2)
+        part_sum(1, "V")
+        mx_s(1, 3)
+        e_x(1, 0, "A")
+        e_t3(0, 0)
+        sum_mm(1)
+        mx_s(1, 4)
+        sum_out(1, "A")
+        mx_s(1, 5)
+        quant_e(0, 1)
+        mx_s(1, 6)
+        e_z(1, 0, "V")
+        mx_s(1, 7)
+        e_x(1, 1, "A")
+        quant_e(0, 0)
+        e_t3(1, 0)
+        mx_y(0, 0, 0)
+        e_z(1, 1, "A")
+        mx_y(0, 1, 0)
+        mx_y(0, 0, 1)
+        quant_e(1, 0)
+        y_evac(0, 0, 0, "A")
+        e_t3(1, 1)
+        y_evac(0, 1, 0, "A")
+        mx_y(0, 1, 1)
+        y_evac(0, 0, 1, "A")
+        y_store_half(1, 0)
+        quant_e(1, 1)
+        mx_y(1, 0, 0)
+        y_evac(0, 1, 1, "V")
+        y_store_half(0, 1)
+        y_store_half(0, 0)
+        mx_y(1, 1, 0)
+        y_evac(1, 0, 0, "V")
+        y_store_half(1, 1)
+        mx_y(1, 0, 1)
+        y_evac(1, 1, 0, "A")
+        y_store_half(2, 0)
+        mx_y(1, 1, 1)
+        y_evac(1, 0, 1, "A")
+        y_mix(1, "V")
+        y_evac(1, 1, 1, "A")
+        y_store_half(2, 1)
+        y_mix(0, "V")
+        y_store_half(3, 1)
+        y_mix(3, "A")
+        y_quant(1)
+        y_store_half(3, 0)
+        y_mix(2, "V")
+        y_quant(0)
+        y_quant(2)
+        words_store(0)
+        y_quant(3)
+        words_store(1)
+        scales_store()

@@ -32,10 +32,12 @@ def tile_weighteddifferentialghostimage_x1_kernel(tc, t, i1, r, q, i2, out_0, ou
         t_v = t.rearrange("(p s) n -> p s n", s=4)
         i1_v = i1.rearrange("(g p s) n -> g p s n", g=2, s=4)
         i2_v = i2.rearrange("(g p j) c -> g p j c", g=2, j=4)
-        q_b = keep.tile([P, 2, 4], BF16, name="q_b")
-        r_b = keep.tile([P, 2, 4], BF16, name="r_b")
-        nc.scalar.dma_start(out=r_b[:], in_=r.rearrange("(g p s) -> p g s", g=2, s=4))
-        nc.scalar.dma_start(out=q_b[:], in_=q.rearrange("(g p s) -> p g s", g=2, s=4))
+        warm = keep.tile([P, 512], BF16, name="warm", align_bytes=64)
+        nc.vector.memset(warm[:], 0.0)
+        rows = keep.tile([P, 512], BF16, name="rows", align_bytes=64)
+        nc.vector.memset(rows[:], 0.0)
+        nc.scalar.dma_start(out=rows[0:2, :], in_=r.rearrange("(g k) -> g k", g=2))
+        nc.scalar.dma_start(out=rows[2:4, :], in_=q.rearrange("(g k) -> g k", g=2))
 
         t_sb = [None] * 4
         i1_sb = [None] * 4
@@ -154,7 +156,8 @@ def tile_weighteddifferentialghostimage_x1_kernel(tc, t, i1, r, q, i2, out_0, ou
 
         def mix_i2h(a, half, engine):
             cols = slice(256 * half, 256 * half + 256)
-            copy(engine, i2_grp[a][:, cols, :], i2_sb[a][:, :, cols].rearrange("p j c -> p c j"))
+            dst = i2_grp[a][:, cols, :].rearrange("p (c i) j -> p c j i", i=4)
+            copy(engine, dst, i2_sb[a][:, :, cols].rearrange("p j (c i) -> p c j i", i=4))
 
         def quant_i2(a):
             cols = slice(512 * (a % 2), 512 * (a % 2) + 512)
@@ -222,9 +225,24 @@ def tile_weighteddifferentialghostimage_x1_kernel(tc, t, i1, r, q, i2, out_0, ou
         w_neg = keep.tile([P, 8], F32, name="w_neg")
         r_bank = []
 
+        rq_bank = []
+        rq = keep.tile([P, 16], BF16, name="rq", align_bytes=64)
+
+        def dummy(k):
+            bank = psum_m.tile([P, 512], F32, name="bank_w", tag="m")
+            for i in range(k):
+                nc.tensor.matmul(bank[:], lhsT=warm[:, :P], rhs=warm[:], start=True, stop=True)
+
+        def consts_t():
+            bank = psum_tr.tile([P, 4, P], F32, name="bank_tr", tag="tr")
+            rq_bank.append(bank)
+            for u in range(2):
+                nc.tensor.transpose(bank[:, u, :], rows[:].bitcast(F32)[:, u:256:2], ident[:])
+
         def consts_a(engine):
-            copy(engine, q_f[:], q_b[:].rearrange("p g s -> p (g s)"))
-            copy(engine, r_f[:], r_b[:].rearrange("p g s -> p (g s)"))
+            copy(engine, rq[:].bitcast(F32).rearrange("p (x u) -> p x u", u=2), rq_bank[0][:, 0:2, 0:4].rearrange("p u x -> p x u"))
+            copy(engine, r_f[:], rq[:, 0:8])
+            copy(engine, q_f[:], rq[:, 8:16])
 
         def consts_mm():
             r_bank.append(psum_tr.tile([P, 4, P], F32, name="bank_tr", tag="tr"))
@@ -330,10 +348,7 @@ def tile_weighteddifferentialghostimage_x1_kernel(tc, t, i1, r, q, i2, out_0, ou
 
         def y_mix(c, engine):
             src = y_sb[:, :, 256 * c : 256 * c + 256].rearrange("p s c -> p c s")
-            if engine == "A":
-                nc.scalar.copy(out=y_grp[c][:], in_=src)
-            else:
-                nc.vector.tensor_copy(out=y_grp[c][:], in_=src)
+            copy(engine, y_grp[c][:], src)
 
         def y_quant(c):
             cols = slice(256 * c, 256 * c + 256)
@@ -348,7 +363,7 @@ def tile_weighteddifferentialghostimage_x1_kernel(tc, t, i1, r, q, i2, out_0, ou
         def scales_store():
             dst = out_2[0].bitcast(I32)
             for k in range(4):
-                eng = nc.scalar if k % 2 == 0 else nc.sync
+                eng = nc.scalar
                 eng.dma_start(out=dst[4 * k : 4 * k + 4, :], in_=y_scales[32 * k : 32 * k + 4, :].bitcast(I32))
 
         for h in range(len(BLOCKS)):
@@ -376,135 +391,137 @@ def tile_weighteddifferentialghostimage_x1_kernel(tc, t, i1, r, q, i2, out_0, ou
         load_t(3)
         load_i2(2)
         load_i2(3)
-        consts_a("V")
-        consts_mm()
+        dummy(4)
         turn_t(0)
-        consts_b()
         turn_t(1)
-        evac_t1(0, "A")
-        turn_i1s(0)
+        evac_t1(0, "V")
+        dummy(2)
         evac_t1(1, "A")
-        turn_i1s(1)
-        evac_i1s(0, "V")
-        turn_i1s(2)
-        evac_i1s(1, "A")
+        turn_i1s(0)
         quant_t(0)
+        turn_i1s(1)
+        evac_i1s(0, "A")
+        dummy(2)
+        evac_i1s(1, "A")
+        turn_i1s(2)
         turn_i1s(3)
+        mix_i2h(0, 1, "V")
         evac_i1s(2, "A")
         quant_i1(0)
-        evac_i1s(3, "A")
+        evac_i1s(3, "V")
         mx_mean(0, 0)
         mx_s(0, 0)
-        mix_i2h(0, 1, "A")
-        quant_i1(1)
-        mx_mean(0, 1)
-        mx_s(0, 1)
         mix_i2h(0, 0, "V")
+        mx_mean(0, 1)
+        mix_i2h(1, 1, "A")
+        mx_s(0, 1)
+        quant_i1(1)
         turn_i1s(4)
         turn_i1s(5)
-        mix_i2h(1, 0, "A")
-        evac_i1s(4, "V")
+        mix_i2h(1, 0, "V")
+        evac_i1s(4, "A")
         mx_mean(0, 2)
-        evac_i1s(5, "V")
+        quant_i2(0)
         mx_s(0, 2)
+        evac_i1s(5, "A")
         mx_mean(0, 3)
-        mix_i2h(1, 1, "A")
-        quant_i1(2)
+        quant_i2(1)
         mx_s(0, 3)
         turn_i1s(6)
-        quant_i2(0)
+        quant_i1(2)
         turn_i1s(7)
-        evac_i1s(6, "A")
-        quant_i2(1)
-        mx_mean(0, 4)
-        evac_i1s(7, "A")
-        mx_s(0, 4)
+        mix_i2h(2, 0, "A")
         mix_i2h(2, 1, "V")
+        mx_mean(0, 4)
+        mx_s(0, 4)
+        evac_i1s(7, "V")
         mx_mean(0, 5)
         mx_s(0, 5)
-        quant_i1(3)
-        turn_t(2)
-        mix_i2h(3, 1, "A")
-        mix_i2h(2, 0, "V")
-        turn_t(3)
-        mx_mean(0, 6)
         mix_i2h(3, 0, "V")
-        mx_s(0, 6)
+        evac_i1s(6, "A")
+        consts_t()
+        quant_i2(2)
+        consts_a("A")
+        turn_t(2)
+        quant_i1(3)
+        turn_t(3)
         evac_t1(2, "A")
+        consts_mm()
+        mix_i2h(3, 1, "V")
+        mx_mean(0, 6)
+        evac_t1(3, "A")
+        mx_s(0, 6)
+        consts_b()
         mx_mean(0, 7)
-        evac_t1(3, "V")
         mx_s(0, 7)
         part_sum(0, "A")
-        quant_i2(3)
-        sum_mm(0)
         quant_t(1)
-        sum_out(0, "A")
-        quant_i2(2)
         e_x(0, 1, "A")
+        sum_mm(0)
+        quant_i2(3)
         mx_mean(1, 0)
         mx_mean(1, 1)
-        e_z(0, 1, "V")
+        sum_out(0, "V")
         mx_mean(1, 2)
+        e_z(0, 1, "A")
         mx_mean(1, 3)
+        e_u1(0, 0)
         mx_mean(1, 4)
-        e_z(0, 0, "V")
-        e_x(0, 0, "A")
         mx_mean(1, 5)
         mx_mean(1, 6)
-        e_t3(0, 1)
         mx_mean(1, 7)
+        e_u2(0, 0)
         mx_s(1, 0)
+        part_sum(1, "A")
         mx_s(1, 1)
         mx_s(1, 2)
-        part_sum(1, "V")
         mx_s(1, 3)
-        e_x(1, 0, "A")
-        e_t3(0, 0)
+        e_t3(0, 1)
         sum_mm(1)
         mx_s(1, 4)
-        sum_out(1, "A")
         mx_s(1, 5)
-        quant_e(0, 1)
-        mx_s(1, 6)
-        e_z(1, 0, "V")
-        mx_s(1, 7)
-        e_x(1, 1, "A")
+        sum_out(1, "A")
         quant_e(0, 0)
-        e_t3(1, 0)
-        mx_y(0, 0, 0)
+        mx_s(1, 6)
+        quant_e(0, 1)
         e_z(1, 1, "A")
+        mx_s(1, 7)
+        e_u1(1, 0)
+        mx_y(0, 0, 0)
         mx_y(0, 1, 0)
+        e_x(1, 1, "A")
         mx_y(0, 0, 1)
-        quant_e(1, 0)
+        e_u2(1, 0)
         y_evac(0, 0, 0, "A")
         e_t3(1, 1)
-        y_evac(0, 1, 0, "A")
-        mx_y(0, 1, 1)
         y_evac(0, 0, 1, "A")
-        y_store_half(1, 0)
-        quant_e(1, 1)
-        mx_y(1, 0, 0)
-        y_evac(0, 1, 1, "V")
-        y_store_half(0, 1)
         y_store_half(0, 0)
+        mx_y(0, 1, 1)
+        y_evac(0, 1, 0, "A")
+        quant_e(1, 0)
+        y_store_half(0, 1)
+        quant_e(1, 1)
+        y_evac(0, 1, 1, "A")
+        y_store_half(1, 0)
+        mx_y(1, 0, 0)
+        y_store_half(1, 1)
         mx_y(1, 1, 0)
         y_evac(1, 0, 0, "V")
-        y_store_half(1, 1)
         mx_y(1, 0, 1)
         y_evac(1, 1, 0, "A")
         y_store_half(2, 0)
         mx_y(1, 1, 1)
         y_evac(1, 0, 1, "A")
-        y_mix(1, "V")
+        y_store_half(3, 0)
+        y_mix(0, "V")
         y_evac(1, 1, 1, "A")
         y_store_half(2, 1)
-        y_mix(0, "V")
+        y_mix(1, "V")
         y_store_half(3, 1)
-        y_mix(3, "A")
-        y_quant(1)
-        y_store_half(3, 0)
-        y_mix(2, "V")
         y_quant(0)
+        y_mix(3, "A")
+        y_mix(2, "V")
+        y_quant(1)
         y_quant(2)
         words_store(0)
         y_quant(3)

@@ -36,25 +36,33 @@ def tile_weighteddifferentialghostimage_x1_kernel(tc, t, i1, r, q, i2, out_0, ou
         nc.vector.memset(warm[:], 0.0)
         rows = keep.tile([P, 512], BF16, name="rows", align_bytes=64)
         nc.vector.memset(rows[:], 0.0)
-        nc.scalar.dma_start(out=rows[0:2, :], in_=r.rearrange("(g k) -> g k", g=2))
-        nc.scalar.dma_start(out=rows[2:4, :], in_=q.rearrange("(g k) -> g k", g=2))
 
         t_sb = [None] * 4
         i1_sb = [None] * 4
         i2_sb = [None] * 4
 
         def load_t(s):
-            t_sb[s] = keep.tile([P, N], BF16, name="t_sb%d" % s, align_bytes=64)
-            nc.sync.dma_start(out=t_sb[s][:], in_=t_v[:, s, :])
+            one = keep.tile([P, N], BF16, name="t_sb%d" % s, align_bytes=64)
+            nc.sync.dma_start(out=one[:], in_=t_v[:, s, :])
+            t_sb[s] = one[:]
 
         def load_i1(a):
             i1_sb[a] = keep.tile([P, 2, N], BF16, name="i1_sb%d" % a, align_bytes=64)
             nc.sync.dma_start(out=i1_sb[a][:], in_=i1_v[a // 2][:, 2 * (a % 2) : 2 * (a % 2) + 2, :])
 
-        def load_i2(a):
-            i2_sb[a] = keep.tile([P, 4, 512], BF16, name="i2_sb%d" % a, align_bytes=64)
-            nc.sync.dma_start(out=i2_sb[a][:], in_=i2_v[a // 2][:, :, 512 * (a % 2) : 512 * (a % 2) + 512])
+        def load_i2(g):
+            i2_sb[g] = keep.tile([P, 4, C], BF16, name="i2_sb%d" % g, align_bytes=64)
+            nc.sync.dma_start(out=i2_sb[g][:], in_=i2_v[g])
 
+        def load_rq():
+            nc.sync.dma_start(out=rows[0:2, :], in_=r.rearrange("(g k) -> g k", g=2))
+            nc.sync.dma_start(out=rows[2:4, :], in_=q.rearrange("(g k) -> g k", g=2))
+
+        def load_t2(s):
+            pair = keep.tile([P, 2, N], BF16, name="t_sb%d" % s, align_bytes=64)
+            nc.sync.dma_start(out=pair[:], in_=t_v[:, s : s + 2, :])
+            t_sb[s] = pair[:, 0, :]
+            t_sb[s + 1] = pair[:, 1, :]
 
         ident = keep.tile([P, P], F32, name="ident")
         make_identity(nc, ident[:])
@@ -94,7 +102,7 @@ def tile_weighteddifferentialghostimage_x1_kernel(tc, t, i1, r, q, i2, out_0, ou
             return P * BLOCKS[h][1]
 
         def turn_t(s):
-            t_bank[s] = turn(t_sb[s][:])
+            t_bank[s] = turn(t_sb[s])
 
         def evac_t(h, engines):
             s0, ns = BLOCKS[h]
@@ -156,8 +164,9 @@ def tile_weighteddifferentialghostimage_x1_kernel(tc, t, i1, r, q, i2, out_0, ou
 
         def mix_i2h(a, half, engine):
             cols = slice(256 * half, 256 * half + 256)
+            cin = slice(512 * (a % 2) + 256 * half, 512 * (a % 2) + 256 * half + 256)
             dst = i2_grp[a][:, cols, :].rearrange("p (c i) j -> p c j i", i=4)
-            copy(engine, dst, i2_sb[a][:, :, cols].rearrange("p j (c i) -> p c j i", i=4))
+            copy(engine, dst, i2_sb[a // 2][:, :, cin].rearrange("p j (c i) -> p c j i", i=4))
 
         def quant_i2(a):
             cols = slice(512 * (a % 2), 512 * (a % 2) + 512)
@@ -183,7 +192,7 @@ def tile_weighteddifferentialghostimage_x1_kernel(tc, t, i1, r, q, i2, out_0, ou
 
         def mx_s(h, j):
             per = 4 // BLOCKS[h][1]
-            if j % per == 0:
+            if (h, j // per) not in s_bank:
                 s_bank[(h, j // per)] = psum_s.tile([P, 512], F32, name="bank_s", tag="s")
             for g in range(2):
                 mx1(s_of(h, j), j, h, g, g == 0, g == 1)
@@ -304,6 +313,28 @@ def tile_weighteddifferentialghostimage_x1_kernel(tc, t, i1, r, q, i2, out_0, ou
                 op=ADD,
             )
 
+        def e_u2s(h, g, s):
+            cols = slice(P * s, P * s + P)
+            nc.vector.tensor_tensor(
+                out=e_out(h, g)[:, cols, :],
+                in0=d_sb[(h, g)][:, :, cols].rearrange("p k b -> p b k"),
+                in1=q_f[:, 4 * g : 4 * g + 4].unsqueeze(1).to_broadcast([P, P, 4]),
+                op=MULT,
+            )
+
+        def e_t3s(h, g, s):
+            cols = slice(P * s, P * s + P)
+            nc.vector.tensor_tensor(
+                out=e_out(h, g)[:, cols, :],
+                in0=d_sb[(h, g)][:, :, cols].rearrange("p k b -> p b k"),
+                in1=z_sb[(h, g)][:, :, cols].rearrange("p k b -> p b k"),
+                op=ADD,
+            )
+
+        def quant_es(h, g, s):
+            cols = slice(P * s, P * s + P)
+            quant(e_grp[(h, g)][:, 4 * P * s : 4 * P * s + 4 * P], e_codes[h][:, g, cols], e_scales[h][:, g, cols])
+
         def quant_e(h, g):
             quant(e_grp[(h, g)][:], e_codes[h][:, g, :], e_scales[h][:, g, :])
 
@@ -311,12 +342,12 @@ def tile_weighteddifferentialghostimage_x1_kernel(tc, t, i1, r, q, i2, out_0, ou
         y_bank = {}
 
         def mx_y(h, s, c):
-            y_bank[(h, s, c)] = psum_tr.tile([P, 4, P], F32, name="bank_tr", tag="tr")
+            y_bank[(h, s, c)] = psum_tr.tile([P, 512], F32, name="bank_y0", tag="tr")
             cols = slice(512 * c, 512 * c + 512)
             rows = slice(P * s, P * s + P)
             for g in range(2):
                 nc.tensor.matmul_mx(
-                    out=y_bank[(h, s, c)][:].rearrange("p a b -> p (a b)"),
+                    out=y_bank[(h, s, c)][:],
                     lhsT=e_codes[h][:, g, rows].bitcast(FP8X4),
                     lhsT_scale=e_scales[h][:, g, rows],
                     rhs=i2_codes[:, g, cols].bitcast(FP8X4),
@@ -325,8 +356,23 @@ def tile_weighteddifferentialghostimage_x1_kernel(tc, t, i1, r, q, i2, out_0, ou
                     stop=g == 1,
                 )
 
+        def mx_yg(h, s, c, g):
+            if g == 0:
+                y_bank[(h, s, c)] = psum_s.tile([P, 512], F32, name="bank_y", tag="s")
+            cols = slice(512 * c, 512 * c + 512)
+            rows_s = slice(P * s, P * s + P)
+            nc.tensor.matmul_mx(
+                out=y_bank[(h, s, c)][:],
+                lhsT=e_codes[h][:, g, rows_s].bitcast(FP8X4),
+                lhsT_scale=e_scales[h][:, g, rows_s],
+                rhs=i2_codes[:, g, cols].bitcast(FP8X4),
+                rhs_scale=i2_scales[:, g, cols],
+                start=g == 0,
+                stop=g == 1,
+            )
+
         def y_evac(h, s, c, engine):
-            src = y_bank[(h, s, c)][:].rearrange("p a b -> p (a b)")
+            src = y_bank[(h, s, c)][:]
             dst = y_sb[:, BLOCKS[h][0] + s, 512 * c : 512 * c + 512]
             if engine == "A":
                 nc.scalar.mul(dst, src, 1.0 / 32.0)
@@ -382,146 +428,155 @@ def tile_weighteddifferentialghostimage_x1_kernel(tc, t, i1, r, q, i2, out_0, ou
         load_t(0)
         load_t(1)
         load_i1(0)
+        dummy(1)
+        load_rq()
         load_i1(1)
+        dummy(4)
         load_i2(0)
         load_i1(2)
-        load_i2(1)
         load_i1(3)
-        load_t(2)
-        load_t(3)
-        load_i2(2)
-        load_i2(3)
-        dummy(4)
+        load_i2(1)
+        load_t2(2)
+        dummy(1)
         turn_t(0)
         turn_t(1)
-        evac_t1(0, "V")
-        dummy(2)
+        evac_t1(0, "A")
+        dummy(1)
+        dummy(1)
         evac_t1(1, "A")
-        turn_i1s(0)
-        quant_t(0)
         turn_i1s(1)
-        evac_i1s(0, "A")
-        dummy(2)
+        quant_t(0)
+        turn_i1s(0)
         evac_i1s(1, "A")
-        turn_i1s(2)
         turn_i1s(3)
-        mix_i2h(0, 1, "V")
-        evac_i1s(2, "A")
+        evac_i1s(0, "V")
+        dummy(1)
+        dummy(1)
+        evac_i1s(3, "A")
+        turn_i1s(2)
         quant_i1(0)
-        evac_i1s(3, "V")
+        mx_s(0, 1)
+        mix_i2h(0, 1, "V")
+        mix_i2h(1, 0, "A")
         mx_mean(0, 0)
         mx_s(0, 0)
-        mix_i2h(0, 0, "V")
-        mx_mean(0, 1)
-        mix_i2h(1, 1, "A")
-        mx_s(0, 1)
-        quant_i1(1)
+        evac_i1s(2, "V")
         turn_i1s(4)
+        mix_i2h(0, 0, "V")
+        mix_i2h(1, 1, "A")
         turn_i1s(5)
-        mix_i2h(1, 0, "V")
+        quant_i1(1)
+        mx_mean(0, 1)
         evac_i1s(4, "A")
-        mx_mean(0, 2)
-        quant_i2(0)
-        mx_s(0, 2)
-        evac_i1s(5, "A")
-        mx_mean(0, 3)
         quant_i2(1)
-        mx_s(0, 3)
+        mx_s(0, 2)
+        turn_i1s(7)
+        evac_i1s(5, "A")
+        quant_i2(0)
         turn_i1s(6)
         quant_i1(2)
-        turn_i1s(7)
-        mix_i2h(2, 0, "A")
+        evac_i1s(7, "A")
+        mx_mean(0, 2)
         mix_i2h(2, 1, "V")
-        mx_mean(0, 4)
-        mx_s(0, 4)
-        evac_i1s(7, "V")
-        mx_mean(0, 5)
-        mx_s(0, 5)
-        mix_i2h(3, 0, "V")
+        mx_mean(0, 3)
         evac_i1s(6, "A")
+        mx_mean(0, 4)
         consts_t()
-        quant_i2(2)
-        consts_a("A")
+        mix_i2h(2, 0, "V")
+        mix_i2h(3, 1, "A")
         turn_t(2)
         quant_i1(3)
         turn_t(3)
+        mix_i2h(3, 0, "V")
         evac_t1(2, "A")
-        consts_mm()
-        mix_i2h(3, 1, "V")
-        mx_mean(0, 6)
-        evac_t1(3, "A")
+        mx_mean(0, 5)
         mx_s(0, 6)
-        consts_b()
+        quant_i2(2)
+        evac_t1(3, "A")
+        mx_mean(0, 6)
         mx_mean(0, 7)
-        mx_s(0, 7)
-        part_sum(0, "A")
+        consts_a("A")
         quant_t(1)
-        e_x(0, 1, "A")
-        sum_mm(0)
+        mx_s(0, 5)
+        mx_s(0, 3)
+        e_x(0, 0, "A")
+        consts_mm()
+        part_sum(0, "V")
+        mx_s(0, 4)
         quant_i2(3)
+        mx_s(0, 7)
+        sum_mm(0)
+        consts_b()
+        e_x(0, 1, "A")
         mx_mean(1, 0)
         mx_mean(1, 1)
-        sum_out(0, "V")
         mx_mean(1, 2)
-        e_z(0, 1, "A")
+        sum_out(0, "V")
         mx_mean(1, 3)
-        e_u1(0, 0)
+        e_z(0, 1, "V")
         mx_mean(1, 4)
+        e_z(0, 0, "A")
         mx_mean(1, 5)
         mx_mean(1, 6)
         mx_mean(1, 7)
-        e_u2(0, 0)
-        mx_s(1, 0)
-        part_sum(1, "A")
-        mx_s(1, 1)
-        mx_s(1, 2)
-        mx_s(1, 3)
         e_t3(0, 1)
+        mx_s(1, 1)
+        mx_s(1, 6)
+        mx_s(1, 2)
+        part_sum(1, "A")
+        mx_s(1, 7)
+        e_t3(0, 0)
         sum_mm(1)
         mx_s(1, 4)
-        mx_s(1, 5)
-        sum_out(1, "A")
-        quant_e(0, 0)
-        mx_s(1, 6)
+        mx_s(1, 0)
         quant_e(0, 1)
-        e_z(1, 1, "A")
-        mx_s(1, 7)
-        e_u1(1, 0)
-        mx_y(0, 0, 0)
-        mx_y(0, 1, 0)
+        sum_out(1, "A")
+        mx_s(1, 5)
+        quant_e(0, 0)
         e_x(1, 1, "A")
+        mx_s(1, 3)
+        e_u1(1, 0)
         mx_y(0, 0, 1)
-        e_u2(1, 0)
-        y_evac(0, 0, 0, "A")
-        e_t3(1, 1)
-        y_evac(0, 0, 1, "A")
-        y_store_half(0, 0)
+        mx_y(0, 1, 0)
+        y_evac(0, 0, 1, "V")
+        e_z(1, 1, "A")
         mx_y(0, 1, 1)
-        y_evac(0, 1, 0, "A")
+        e_u2(1, 0)
+        mx_y(0, 0, 0)
+        e_t3s(1, 1, 0)
+        y_evac(0, 0, 0, "A")
         quant_e(1, 0)
-        y_store_half(0, 1)
-        quant_e(1, 1)
+        y_evac(0, 1, 0, "A")
+        y_store_half(0, 0)
+        e_t3s(1, 1, 1)
+        mx_yg(1, 0, 0, 0)
         y_evac(0, 1, 1, "A")
-        y_store_half(1, 0)
-        mx_y(1, 0, 0)
+        mx_yg(1, 1, 0, 0)
+        quant_es(1, 1, 0)
+        quant_es(1, 1, 1)
+        mx_yg(1, 0, 0, 1)
         y_store_half(1, 1)
-        mx_y(1, 1, 0)
-        y_evac(1, 0, 0, "V")
-        mx_y(1, 0, 1)
-        y_evac(1, 1, 0, "A")
+        y_store_half(0, 1)
+        y_store_half(1, 0)
+        mx_yg(1, 1, 0, 1)
+        mx_yg(1, 0, 1, 0)
+        y_evac(1, 0, 0, "A")
+        mx_yg(1, 0, 1, 1)
+        y_evac(1, 1, 0, "V")
+        mx_yg(1, 1, 1, 0)
+        mx_yg(1, 1, 1, 1)
         y_store_half(2, 0)
-        mx_y(1, 1, 1)
         y_evac(1, 0, 1, "A")
-        y_store_half(3, 0)
-        y_mix(0, "V")
+        y_mix(1, "V")
         y_evac(1, 1, 1, "A")
         y_store_half(2, 1)
-        y_mix(1, "V")
-        y_store_half(3, 1)
-        y_quant(0)
+        y_mix(0, "V")
+        y_store_half(3, 0)
         y_mix(3, "A")
-        y_mix(2, "V")
+        y_store_half(3, 1)
         y_quant(1)
+        y_mix(2, "V")
+        y_quant(0)
         y_quant(2)
         words_store(0)
         y_quant(3)

@@ -51,8 +51,14 @@ def tile_weighteddifferentialghostimage_x1_kernel(tc, t, i1, r, q, i2, out_0, ou
             nc.sync.dma_start(out=i1_sb[a][:], in_=i1_v[a // 2][:, 2 * (a % 2) : 2 * (a % 2) + 2, :])
 
         def load_i2(g):
-            i2_sb[g] = keep.tile([P, 4, C], BF16, name="i2_sb%d" % g, align_bytes=64)
-            nc.sync.dma_start(out=i2_sb[g][:], in_=i2_v[g])
+            i2_sb[g] = keep.tile([P, 4, 512], BF16, name="i2_sb%d" % g, align_bytes=64)
+            nc.sync.dma_start(out=i2_sb[g][:], in_=i2_v[g // 2][:, :, 512 * (g % 2) : 512 * (g % 2) + 512])
+
+        def load_i1s(j):
+            a = j // 2
+            if i1_sb[a] is None:
+                i1_sb[a] = keep.tile([P, 2, N], BF16, name="i1_sb%d" % a, align_bytes=64)
+            nc.sync.dma_start(out=i1_sb[a][:, j % 2, :], in_=i1_v[a // 2][:, 2 * (a % 2) + j % 2, :])
 
         def load_rq():
             nc.sync.dma_start(out=rows[0:2, :], in_=r.rearrange("(g k) -> g k", g=2))
@@ -145,9 +151,11 @@ def tile_weighteddifferentialghostimage_x1_kernel(tc, t, i1, r, q, i2, out_0, ou
             dst = i1_grp[a][:].bitcast(F32).rearrange("p (s g r u) -> p s g r u", s=2, g=2, u=2)
             evac(engine, dst[:, j % 2], i1_bank[j])
 
+        def quant_i1s(j):
+            a, s = j // 2, j % 2
+            quant(i1_grp[a][:, 1024 * s : 1024 * s + 1024], i1_codes[a][:, s].rearrange("p g r -> p (g r)"), i1_scales[a][:, s].rearrange("p g r -> p (g r)"))
+
         def quant_i1(a):
-            i1_codes[a] = keep.tile([P, 2, 2, P], U32, name="i1_codes%d" % a, align_bytes=64)
-            i1_scales[a] = keep.tile([P, 2, 2, P], U8, name="i1_scales%d" % a, align_bytes=64)
             quant(i1_grp[a][:], i1_codes[a][:].rearrange("p s g r -> p (s g r)"), i1_scales[a][:].rearrange("p s g r -> p (s g r)"))
 
         i2_codes = keep.tile([P, 2, C], U32, name="i2_codes", align_bytes=64)
@@ -164,9 +172,8 @@ def tile_weighteddifferentialghostimage_x1_kernel(tc, t, i1, r, q, i2, out_0, ou
 
         def mix_i2h(a, half, engine):
             cols = slice(256 * half, 256 * half + 256)
-            cin = slice(512 * (a % 2) + 256 * half, 512 * (a % 2) + 256 * half + 256)
             dst = i2_grp[a][:, cols, :].rearrange("p (c i) j -> p c j i", i=4)
-            copy(engine, dst, i2_sb[a // 2][:, :, cin].rearrange("p j (c i) -> p c j i", i=4))
+            copy(engine, dst, i2_sb[a][:, :, cols].rearrange("p j (c i) -> p c j i", i=4))
 
         def quant_i2(a):
             cols = slice(512 * (a % 2), 512 * (a % 2) + 512)
@@ -322,6 +329,15 @@ def tile_weighteddifferentialghostimage_x1_kernel(tc, t, i1, r, q, i2, out_0, ou
                 op=MULT,
             )
 
+        def e_zp(h, g, engine):
+            for k in range(4):
+                j = 4 * g + k
+                src = total[h][:].rearrange("p a b -> p (a b)")[:, : width(h)]
+                if engine == "A":
+                    nc.scalar.activation(out=z_sb[(h, g)][:, k, :], in_=src, func=COPY, scale=w_neg[:, j : j + 1])
+                else:
+                    nc.vector.tensor_scalar_mul(z_sb[(h, g)][:, k, :], src, w_neg[:, j : j + 1])
+
         def e_t3s(h, g, s):
             cols = slice(P * s, P * s + P)
             nc.vector.tensor_tensor(
@@ -406,6 +422,10 @@ def tile_weighteddifferentialghostimage_x1_kernel(tc, t, i1, r, q, i2, out_0, ou
             cols = slice(512 * c, 512 * c + 512)
             nc.sync.dma_start(out=words_v[:, cols], in_=y_codes[:, cols].bitcast(I32))
 
+        def words_store4(c):
+            cols = slice(256 * c, 256 * c + 256)
+            nc.sync.dma_start(out=words_v[:, cols], in_=y_codes[:, cols].bitcast(I32))
+
         def scales_store():
             dst = out_2[0].bitcast(I32)
             for k in range(4):
@@ -421,164 +441,170 @@ def tile_weighteddifferentialghostimage_x1_kernel(tc, t, i1, r, q, i2, out_0, ou
                 z_sb[(h, g)] = keep.tile([P, 4, width(h)], F32, name="z_sb%d_%d" % (h, g), align_bytes=64)
                 e_grp[(h, g)] = keep.tile([P, width(h) * 4], BF16, name="e_grp%d_%d" % (h, g), align_bytes=64)
         for a in range(4):
+            i1_codes[a] = keep.tile([P, 2, 2, P], U32, name="i1_codes%d" % a, align_bytes=64)
+            i1_scales[a] = keep.tile([P, 2, 2, P], U8, name="i1_scales%d" % a, align_bytes=64)
             i1_grp[a] = keep.tile([P, 2 * 1024], BF16, name="i1_grp%d" % a, align_bytes=64)
             i2_grp[a] = keep.tile([P, 512, 4], BF16, name="i2_grp%d" % a, align_bytes=64)
             y_grp[a] = keep.tile([P, 256, 4], BF16, name="y_grp%d" % a, align_bytes=64)
 
-        load_t(0)
         load_t(1)
+        load_t(0)
         load_i1(0)
-        dummy(1)
+        dummy(4)
         load_rq()
         load_i1(1)
-        dummy(4)
-        load_i2(0)
+        load_i2(3)
         load_i1(2)
+        load_i2(2)
         load_i1(3)
-        load_i2(1)
+        load_i2(0)
         load_t2(2)
+        load_i2(1)
         dummy(1)
-        turn_t(0)
+        dummy(1)
         turn_t(1)
+        turn_t(0)
+        evac_t1(1, "V")
+        dummy(1)
+        dummy(1)
         evac_t1(0, "A")
-        dummy(1)
-        dummy(1)
-        evac_t1(1, "A")
-        turn_i1s(1)
-        quant_t(0)
         turn_i1s(0)
-        evac_i1s(1, "A")
-        turn_i1s(3)
-        evac_i1s(0, "V")
+        quant_t(0)
+        turn_i1s(1)
+        evac_i1s(0, "A")
+        consts_t()
         dummy(1)
+        evac_i1s(1, "V")
         dummy(1)
-        evac_i1s(3, "A")
         turn_i1s(2)
         quant_i1(0)
-        mx_s(0, 1)
-        mix_i2h(0, 1, "V")
-        mix_i2h(1, 0, "A")
+        mix_i2h(3, 0, "A")
+        turn_i1s(3)
+        mix_i2h(3, 1, "V")
         mx_mean(0, 0)
-        mx_s(0, 0)
-        evac_i1s(2, "V")
-        turn_i1s(4)
-        mix_i2h(0, 0, "V")
-        mix_i2h(1, 1, "A")
-        turn_i1s(5)
-        quant_i1(1)
         mx_mean(0, 1)
-        evac_i1s(4, "A")
-        quant_i2(1)
-        mx_s(0, 2)
+        consts_a("A")
+        evac_i1s(2, "V")
+        turn_i1s(5)
+        evac_i1s(3, "A")
+        quant_i2(3)
+        turn_i1s(4)
+        mix_i2h(2, 0, "A")
+        quant_i1(1)
+        mx_s(0, 0)
+        evac_i1s(5, "V")
+        mx_s(0, 1)
+        mx_mean(0, 2)
+        mix_i2h(2, 1, "V")
         turn_i1s(7)
-        evac_i1s(5, "A")
-        quant_i2(0)
+        evac_i1s(4, "A")
         turn_i1s(6)
         quant_i1(2)
         evac_i1s(7, "A")
-        mx_mean(0, 2)
-        mix_i2h(2, 1, "V")
         mx_mean(0, 3)
+        mix_i2h(0, 0, "V")
+        consts_mm()
         evac_i1s(6, "A")
         mx_mean(0, 4)
-        consts_t()
-        mix_i2h(2, 0, "V")
-        mix_i2h(3, 1, "A")
-        turn_t(2)
-        quant_i1(3)
-        turn_t(3)
-        mix_i2h(3, 0, "V")
-        evac_t1(2, "A")
-        mx_mean(0, 5)
-        mx_s(0, 6)
         quant_i2(2)
+        mx_mean(0, 5)
+        mix_i2h(0, 1, "A")
+        turn_t(3)
+        quant_i1(3)
+        turn_t(2)
+        consts_b()
         evac_t1(3, "A")
         mx_mean(0, 6)
         mx_mean(0, 7)
-        consts_a("A")
-        quant_t(1)
-        mx_s(0, 5)
+        evac_t1(2, "A")
+        mx_s(0, 2)
+        quant_i2(0)
         mx_s(0, 3)
+        part_sum(0, "A")
+        mx_s(0, 5)
+        quant_t(1)
         e_x(0, 0, "A")
-        consts_mm()
-        part_sum(0, "V")
-        mx_s(0, 4)
-        quant_i2(3)
-        mx_s(0, 7)
+        mx_s(0, 6)
         sum_mm(0)
-        consts_b()
-        e_x(0, 1, "A")
+        mix_i2h(1, 0, "V")
+        mx_s(0, 4)
         mx_mean(1, 0)
+        mix_i2h(1, 1, "V")
+        sum_out(0, "A")
         mx_mean(1, 1)
         mx_mean(1, 2)
-        sum_out(0, "V")
+        e_z(0, 1, "A")
+        e_z(0, 0, "V")
         mx_mean(1, 3)
-        e_z(0, 1, "V")
         mx_mean(1, 4)
-        e_z(0, 0, "A")
         mx_mean(1, 5)
         mx_mean(1, 6)
-        mx_mean(1, 7)
-        e_t3(0, 1)
-        mx_s(1, 1)
-        mx_s(1, 6)
-        mx_s(1, 2)
-        part_sum(1, "A")
-        mx_s(1, 7)
         e_t3(0, 0)
-        sum_mm(1)
-        mx_s(1, 4)
-        mx_s(1, 0)
-        quant_e(0, 1)
-        sum_out(1, "A")
+        mx_mean(1, 7)
+        mx_s(0, 7)
+        e_x(0, 1, "A")
+        mx_s(1, 6)
         mx_s(1, 5)
+        part_sum(1, "V")
+        mx_s(1, 4)
         quant_e(0, 0)
-        e_x(1, 1, "A")
+        sum_mm(1)
+        quant_i2(1)
+        mx_s(1, 0)
+        e_t3(0, 1)
         mx_s(1, 3)
+        sum_out(1, "A")
+        mx_s(1, 1)
+        mx_s(1, 7)
+        e_x(1, 1, "A")
+        mx_s(1, 2)
         e_u1(1, 0)
-        mx_y(0, 0, 1)
-        mx_y(0, 1, 0)
-        y_evac(0, 0, 1, "V")
         e_z(1, 1, "A")
-        mx_y(0, 1, 1)
+        quant_e(0, 1)
+        mx_y(0, 0, 1)
         e_u2(1, 0)
         mx_y(0, 0, 0)
+        y_evac(0, 0, 1, "A")
+        mx_y(0, 1, 1)
         e_t3s(1, 1, 0)
-        y_evac(0, 0, 0, "A")
-        quant_e(1, 0)
-        y_evac(0, 1, 0, "A")
-        y_store_half(0, 0)
-        e_t3s(1, 1, 1)
-        mx_yg(1, 0, 0, 0)
-        y_evac(0, 1, 1, "A")
-        mx_yg(1, 1, 0, 0)
-        quant_es(1, 1, 0)
-        quant_es(1, 1, 1)
-        mx_yg(1, 0, 0, 1)
-        y_store_half(1, 1)
         y_store_half(0, 1)
-        y_store_half(1, 0)
+        quant_e(1, 0)
+        mx_y(0, 1, 0)
+        y_evac(0, 1, 1, "A")
+        e_t3s(1, 1, 1)
+        mx_yg(1, 1, 0, 0)
+        mx_yg(1, 0, 0, 0)
+        quant_es(1, 1, 0)
+        y_evac(0, 1, 0, "A")
+        y_store_half(1, 1)
+        quant_es(1, 1, 1)
+        y_evac(0, 0, 0, "V")
+        mx_yg(1, 0, 0, 1)
         mx_yg(1, 1, 0, 1)
+        y_store_half(1, 0)
         mx_yg(1, 0, 1, 0)
-        y_evac(1, 0, 0, "A")
+        y_evac(1, 0, 0, "V")
+        y_store_half(0, 0)
         mx_yg(1, 0, 1, 1)
-        y_evac(1, 1, 0, "V")
+        y_evac(1, 1, 0, "A")
         mx_yg(1, 1, 1, 0)
         mx_yg(1, 1, 1, 1)
         y_store_half(2, 0)
         y_evac(1, 0, 1, "A")
-        y_mix(1, "V")
-        y_evac(1, 1, 1, "A")
-        y_store_half(2, 1)
-        y_mix(0, "V")
         y_store_half(3, 0)
+        y_mix(0, "V")
+        y_evac(1, 1, 1, "A")
+        y_mix(1, "V")
         y_mix(3, "A")
         y_store_half(3, 1)
-        y_quant(1)
-        y_mix(2, "V")
         y_quant(0)
+        y_mix(2, "V")
+        words_store4(0)
+        y_store_half(2, 1)
+        y_quant(1)
         y_quant(2)
-        words_store(0)
         y_quant(3)
-        words_store(1)
+        words_store4(2)
+        words_store4(1)
+        words_store4(3)
         scales_store()

from contextlib import ExitStack

import concourse.mybir as mybir
from concourse.masks import make_identity

F32 = mybir.dt.float32
BF16 = mybir.dt.bfloat16
U32 = mybir.dt.uint32
I32 = mybir.dt.int32
U8 = mybir.dt.uint8
FP8X4 = mybir.dt.float8_e4m3fn_x4
ADD = mybir.AluOpType.add
MULT = mybir.AluOpType.mult
COPY = mybir.ActivationFunctionType.Copy

B, N, M, C = 512, 1024, 1024, 1024
FLOPS = 2 * B * N * M + 2 * B * M * C
P = 128
BLOCKS = ((0, 2), (2, 2))


def tile_weighteddifferentialghostimage_x1_kernel(tc, t, i1, r, q, i2, out_0, out_1, out_2):
    nc = tc.nc
    with ExitStack() as ctx:
        keep = ctx.enter_context(tc.tile_pool(name="keep", bufs=1))
        stage = ctx.enter_context(tc.tile_pool(name="stage", bufs=3))
        psum_tr = ctx.enter_context(tc.psum_pool(name="psum_tr", bufs=3))
        psum_s = ctx.enter_context(tc.psum_pool(name="psum_s", bufs=4))
        psum_m = ctx.enter_context(tc.psum_pool(name="psum_m", bufs=1))
        ctx.enter_context(tc.manual_schedule())

        t_v = t.rearrange("(p s) n -> p s n", s=4)
        i1_v = i1.rearrange("(g p s) n -> g p s n", g=2, s=4)
        i2_v = i2.rearrange("(g p j) c -> g p j c", g=2, j=4)
        warm = keep.tile([P, 512], BF16, name="warm", align_bytes=64)
        nc.vector.memset(warm[:], 0.0)
        rows = keep.tile([P, 512], BF16, name="rows", align_bytes=64)
        nc.vector.memset(rows[:], 0.0)

        t_sb = [None] * 4
        i1_sb = [None] * 4
        i2_sb = [None] * 4

        def load_t(s):
            one = keep.tile([P, N], BF16, name="t_sb%d" % s, align_bytes=64)
            nc.sync.dma_start(out=one[:], in_=t_v[:, s, :])
            t_sb[s] = one[:]

        def load_i1(a):
            i1_sb[a] = keep.tile([P, 2, N], BF16, name="i1_sb%d" % a, align_bytes=64)
            nc.sync.dma_start(out=i1_sb[a][:], in_=i1_v[a // 2][:, 2 * (a % 2) : 2 * (a % 2) + 2, :])

        def load_i2(g):
            i2_sb[g] = keep.tile([P, 4, 512], BF16, name="i2_sb%d" % g, align_bytes=64)
            nc.sync.dma_start(out=i2_sb[g][:], in_=i2_v[g // 2][:, :, 512 * (g % 2) : 512 * (g % 2) + 512])

        def load_i1s(j):
            a = j // 2
            if i1_sb[a] is None:
                i1_sb[a] = keep.tile([P, 2, N], BF16, name="i1_sb%d" % a, align_bytes=64)
            nc.sync.dma_start(out=i1_sb[a][:, j % 2, :], in_=i1_v[a // 2][:, 2 * (a % 2) + j % 2, :])

        def load_rq():
            nc.sync.dma_start(out=rows[0:2, :], in_=r.rearrange("(g k) -> g k", g=2))
            nc.sync.dma_start(out=rows[2:4, :], in_=q.rearrange("(g k) -> g k", g=2))

        def load_t2(s):
            pair = keep.tile([P, 2, N], BF16, name="t_sb%d" % s, align_bytes=64)
            nc.sync.dma_start(out=pair[:], in_=t_v[:, s : s + 2, :])
            t_sb[s] = pair[:, 0, :]
            t_sb[s + 1] = pair[:, 1, :]

        ident = keep.tile([P, P], F32, name="ident")
        make_identity(nc, ident[:])
        ones = keep.tile([P, P], F32, name="ones")
        nc.gpsimd.memset(ones[:], 1.0)

        def copy(engine, dst, src):
            if engine == "A":
                nc.scalar.copy(out=dst, in_=src)
            else:
                nc.vector.tensor_copy(out=dst, in_=src)

        def turn(rows):
            bank = psum_tr.tile([P, 4, P], F32, name="bank_tr", tag="tr")
            words = rows.bitcast(F32)
            for g in range(2):
                for u in range(2):
                    nc.tensor.transpose(bank[:, 2 * g + u, :], words[:, 256 * g + u : 256 * (g + 1) : 2], ident[:])
            return bank

        def evac(engine, dst, bank):
            src = bank[:].rearrange("p (g u) r -> p g r u", g=2)
            if engine == "A":
                nc.scalar.copy(out=dst, in_=src)
            else:
                nc.vector.tensor_copy(out=dst, in_=src)

        def quant(src, codes, scales):
            nc.vector.quantize_mx(out=codes.bitcast(FP8X4), scales=scales, in_=src)

        t_codes = {}
        t_scales = {}
        t_grp = {}
        t_bank = {}

        def width(h):
            return P * BLOCKS[h][1]

        def turn_t(s):
            t_bank[s] = turn(t_sb[s])

        def evac_t(h, engines):
            s0, ns = BLOCKS[h]
            t_grp[h] = stage.tile([P, 2 * ns * P * 4], BF16, name="t_grp", tag="t_grp", align_bytes=64)
            dst = t_grp[h][:].bitcast(F32).rearrange("p (g s r u) -> p g s r u", g=2, s=ns, u=2)
            for s in range(ns):
                evac(engines[s], dst[:, :, s], t_bank[s0 + s])

        def evac_t1(s, engine):
            h = [k for k in range(len(BLOCKS)) if BLOCKS[k][0] <= s < BLOCKS[k][0] + BLOCKS[k][1]][0]
            s0, ns = BLOCKS[h]
            dst = t_grp[h][:].bitcast(F32).rearrange("p (g s r u) -> p g s r u", g=2, s=ns, u=2)
            evac(engine, dst[:, :, s - s0], t_bank[s])

        def quant_t(h):
            t_codes[h] = keep.tile([P, 2, width(h)], U32, name="t_codes%d" % h, align_bytes=64)
            t_scales[h] = keep.tile([P, 2, width(h)], U8, name="t_scales%d" % h, align_bytes=64)
            quant(t_grp[h][:], t_codes[h][:].rearrange("p g b -> p (g b)"), t_scales[h][:].rearrange("p g b -> p (g b)"))

        i1_codes = [None] * 4
        i1_scales = [None] * 4
        i1_grp = [None] * 4
        i1_bank = {}

        def turn_i1(a):
            for s in range(2):
                i1_bank[2 * a + s] = turn(i1_sb[a][:, s, :])

        def evac_i1(a, engines):
            i1_grp[a] = stage.tile([P, 2 * 1024], BF16, name="i1_grp", tag="i1_grp", align_bytes=64)
            dst = i1_grp[a][:].bitcast(F32).rearrange("p (s g r u) -> p s g r u", s=2, g=2, u=2)
            for s in range(2):
                evac(engines[s], dst[:, s], i1_bank[2 * a + s])

        def turn_i1s(j):
            i1_bank[j] = turn(i1_sb[j // 2][:, j % 2, :])

        def evac_i1s(j, engine):
            a = j // 2
            dst = i1_grp[a][:].bitcast(F32).rearrange("p (s g r u) -> p s g r u", s=2, g=2, u=2)
            evac(engine, dst[:, j % 2], i1_bank[j])

        def quant_i1s(j):
            a, s = j // 2, j % 2
            quant(i1_grp[a][:, 1024 * s : 1024 * s + 1024], i1_codes[a][:, s].rearrange("p g r -> p (g r)"), i1_scales[a][:, s].rearrange("p g r -> p (g r)"))

        def quant_i1(a):
            quant(i1_grp[a][:], i1_codes[a][:].rearrange("p s g r -> p (s g r)"), i1_scales[a][:].rearrange("p s g r -> p (s g r)"))

        i2_codes = keep.tile([P, 2, C], U32, name="i2_codes", align_bytes=64)
        i2_scales = keep.tile([P, 2, C], U8, name="i2_scales", align_bytes=64)
        i2_grp = [None] * 4

        def mix_i2(a, engine):
            i2_grp[a] = stage.tile([P, 512, 4], BF16, name="i2_grp", tag="i2_grp", align_bytes=64)
            src = i2_sb[a][:].rearrange("p j c -> p c j")
            if engine == "A":
                nc.scalar.copy(out=i2_grp[a][:], in_=src)
            else:
                nc.vector.tensor_copy(out=i2_grp[a][:], in_=src)

        def mix_i2h(a, half, engine):
            cols = slice(256 * half, 256 * half + 256)
            dst = i2_grp[a][:, cols, :].rearrange("p (c i) j -> p c j i", i=4)
            copy(engine, dst, i2_sb[a][:, :, cols].rearrange("p j (c i) -> p c j i", i=4))

        def quant_i2(a):
            cols = slice(512 * (a % 2), 512 * (a % 2) + 512)
            quant(i2_grp[a][:].rearrange("p c j -> p (c j)"), i2_codes[:, a // 2, cols], i2_scales[:, a // 2, cols])

        s_bank = {}
        mean_bank = {}

        def mx1(out, j, h, g, start, stop):
            nc.tensor.matmul_mx(
                out=out,
                lhsT=i1_codes[j // 2][:, j % 2, g, :].bitcast(FP8X4),
                lhsT_scale=i1_scales[j // 2][:, j % 2, g, :],
                rhs=t_codes[h][:, g, :].bitcast(FP8X4),
                rhs_scale=t_scales[h][:, g, :],
                start=start,
                stop=stop,
            )

        def s_of(h, j):
            per = 4 // BLOCKS[h][1]
            return s_bank[(h, j // per)][:, width(h) * (j % per) : width(h) * (j % per + 1)]

        def mx_s(h, j):
            per = 4 // BLOCKS[h][1]
            if (h, j // per) not in s_bank:
                s_bank[(h, j // per)] = psum_s.tile([P, 512], F32, name="bank_s", tag="s")
            for g in range(2):
                mx1(s_of(h, j), j, h, g, g == 0, g == 1)

        def mx_mean(h, j):
            if j == 0:
                mean_bank[h] = psum_m.tile([P, width(h)], F32, name="bank_m", tag="m")
            for g in range(2):
                mx1(mean_bank[h][:], j, h, g, j == 0 and g == 0, j == 7 and g == 1)

        total = {}

        part = {}

        def part_sum(h, engine):
            part[h] = stage.tile([P, width(h)], F32, name="part", tag="part")
            copy(engine, part[h][:], mean_bank[h][:])

        def acc_v(h, j):
            if j == 0:
                part[h] = stage.tile([P, width(h)], F32, name="part", tag="part")
                nc.vector.tensor_copy(out=part[h][:], in_=s_of(h, 0))
            else:
                nc.vector.tensor_tensor(out=part[h][:], in0=part[h][:], in1=s_of(h, j), op=ADD)

        def sum_mm(h):
            total[h] = psum_tr.tile([P, 4, P], F32, name="bank_tr", tag="tr")
            nc.tensor.matmul(total[h][:].rearrange("p a b -> p (a b)")[:, :width(h)], lhsT=ones[:], rhs=part[h][:], start=True, stop=True)

        total_sb = {}

        def sum_out(h, engine):
            total_sb[h] = stage.tile([P, width(h)], F32, name="total_sb", tag="total_sb")
            copy(engine, total_sb[h][:], total[h][:].rearrange("p a b -> p (a b)")[:, : width(h)])

        q_f = keep.tile([P, 8], F32, name="q_f")
        r_f = keep.tile([P, 8], F32, name="r_f")
        r_neg = keep.tile([P, 8], F32, name="r_neg")
        w_neg = keep.tile([P, 8], F32, name="w_neg")
        r_bank = []

        rq_bank = []
        rq = keep.tile([P, 16], BF16, name="rq", align_bytes=64)

        def dummy(k):
            bank = psum_m.tile([P, 512], F32, name="bank_w", tag="m")
            for i in range(k):
                nc.tensor.matmul(bank[:], lhsT=warm[:, :P], rhs=warm[:], start=True, stop=True)

        def consts_t():
            bank = psum_tr.tile([P, 4, P], F32, name="bank_tr", tag="tr")
            rq_bank.append(bank)
            for u in range(2):
                nc.tensor.transpose(bank[:, u, :], rows[:].bitcast(F32)[:, u:256:2], ident[:])

        def consts_a(engine):
            copy(engine, rq[:].bitcast(F32).rearrange("p (x u) -> p x u", u=2), rq_bank[0][:, 0:2, 0:4].rearrange("p u x -> p x u"))
            copy(engine, r_f[:], rq[:, 0:8])
            copy(engine, q_f[:], rq[:, 8:16])

        def consts_mm():
            r_bank.append(psum_tr.tile([P, 4, P], F32, name="bank_tr", tag="tr"))
            nc.tensor.matmul(r_bank[0][:, 0, :8], lhsT=ones[:], rhs=r_f[:], start=True, stop=True)

        def consts_b():
            r_sum = keep.tile([P, 1], F32, name="r_sum")
            r_inv = keep.tile([P, 1], F32, name="r_inv")
            nc.vector.reduce_sum(out=r_sum[:], in_=r_bank[0][:, 0, :8], axis=mybir.AxisListType.X)
            nc.vector.reciprocal(out=r_inv[:], in_=r_sum[:])
            nc.vector.tensor_scalar(out=r_neg[:], in0=r_f[:], scalar1=r_inv[:], scalar2=-1.0, op0=MULT, op1=MULT)
            nc.vector.tensor_mul(out=w_neg[:], in0=r_neg[:], in1=q_f[:])

        e_grp = {}
        e_codes = {}
        e_scales = {}
        d_sb = {}
        z_sb = {}

        def e_u1(h, g):
            for k in range(4):
                j = 4 * g + k
                nc.vector.scalar_tensor_tensor(
                    out=d_sb[(h, g)][:, k, :], in0=total_sb[h][:], scalar=r_neg[:, j : j + 1], in1=s_of(h, j), op0=MULT, op1=ADD
                )

        def e_out(h, g):
            return e_grp[(h, g)][:].rearrange("p (b k) -> p b k", k=4)

        def e_u2(h, g):
            nc.vector.tensor_tensor(
                out=e_out(h, g),
                in0=d_sb[(h, g)][:].rearrange("p k b -> p b k"),
                in1=q_f[:, 4 * g : 4 * g + 4].unsqueeze(1).to_broadcast([P, width(h), 4]),
                op=MULT,
            )

        def e_x(h, g, engine):
            for k in range(4):
                j = 4 * g + k
                if engine == "A":
                    nc.scalar.activation(out=d_sb[(h, g)][:, k, :], in_=s_of(h, j), func=COPY, scale=q_f[:, j : j + 1])
                else:
                    nc.vector.tensor_scalar_mul(d_sb[(h, g)][:, k, :], s_of(h, j), q_f[:, j : j + 1])

        def e_z(h, g, engine):
            for k in range(4):
                j = 4 * g + k
                if engine == "A":
                    nc.scalar.activation(out=z_sb[(h, g)][:, k, :], in_=total_sb[h][:], func=COPY, scale=w_neg[:, j : j + 1])
                else:
                    nc.vector.tensor_scalar_mul(z_sb[(h, g)][:, k, :], total_sb[h][:], w_neg[:, j : j + 1])

        def e_t3(h, g):
            nc.vector.tensor_tensor(
                out=e_out(h, g),
                in0=d_sb[(h, g)][:].rearrange("p k b -> p b k"),
                in1=z_sb[(h, g)][:].rearrange("p k b -> p b k"),
                op=ADD,
            )

        def e_u2s(h, g, s):
            cols = slice(P * s, P * s + P)
            nc.vector.tensor_tensor(
                out=e_out(h, g)[:, cols, :],
                in0=d_sb[(h, g)][:, :, cols].rearrange("p k b -> p b k"),
                in1=q_f[:, 4 * g : 4 * g + 4].unsqueeze(1).to_broadcast([P, P, 4]),
                op=MULT,
            )

        def e_zp(h, g, engine):
            for k in range(4):
                j = 4 * g + k
                src = total[h][:].rearrange("p a b -> p (a b)")[:, : width(h)]
                if engine == "A":
                    nc.scalar.activation(out=z_sb[(h, g)][:, k, :], in_=src, func=COPY, scale=w_neg[:, j : j + 1])
                else:
                    nc.vector.tensor_scalar_mul(z_sb[(h, g)][:, k, :], src, w_neg[:, j : j + 1])

        def e_t3s(h, g, s):
            cols = slice(P * s, P * s + P)
            nc.vector.tensor_tensor(
                out=e_out(h, g)[:, cols, :],
                in0=d_sb[(h, g)][:, :, cols].rearrange("p k b -> p b k"),
                in1=z_sb[(h, g)][:, :, cols].rearrange("p k b -> p b k"),
                op=ADD,
            )

        def quant_es(h, g, s):
            cols = slice(P * s, P * s + P)
            quant(e_grp[(h, g)][:, 4 * P * s : 4 * P * s + 4 * P], e_codes[h][:, g, cols], e_scales[h][:, g, cols])

        def quant_e(h, g):
            quant(e_grp[(h, g)][:], e_codes[h][:, g, :], e_scales[h][:, g, :])

        y_sb = keep.tile([P, 4, C], F32, name="y_sb", align_bytes=64)
        y_bank = {}

        def mx_y(h, s, c):
            y_bank[(h, s, c)] = psum_tr.tile([P, 512], F32, name="bank_y0", tag="tr")
            cols = slice(512 * c, 512 * c + 512)
            rows = slice(P * s, P * s + P)
            for g in range(2):
                nc.tensor.matmul_mx(
                    out=y_bank[(h, s, c)][:],
                    lhsT=e_codes[h][:, g, rows].bitcast(FP8X4),
                    lhsT_scale=e_scales[h][:, g, rows],
                    rhs=i2_codes[:, g, cols].bitcast(FP8X4),
                    rhs_scale=i2_scales[:, g, cols],
                    start=g == 0,
                    stop=g == 1,
                )

        def mx_yg(h, s, c, g):
            if g == 0:
                y_bank[(h, s, c)] = psum_s.tile([P, 512], F32, name="bank_y", tag="s")
            cols = slice(512 * c, 512 * c + 512)
            rows_s = slice(P * s, P * s + P)
            nc.tensor.matmul_mx(
                out=y_bank[(h, s, c)][:],
                lhsT=e_codes[h][:, g, rows_s].bitcast(FP8X4),
                lhsT_scale=e_scales[h][:, g, rows_s],
                rhs=i2_codes[:, g, cols].bitcast(FP8X4),
                rhs_scale=i2_scales[:, g, cols],
                start=g == 0,
                stop=g == 1,
            )

        def y_evac(h, s, c, engine):
            src = y_bank[(h, s, c)][:]
            dst = y_sb[:, BLOCKS[h][0] + s, 512 * c : 512 * c + 512]
            if engine == "A":
                nc.scalar.mul(dst, src, 1.0 / 32.0)
            else:
                nc.vector.tensor_scalar_mul(dst, src, 1.0 / 32.0)

        out_v = out_0.rearrange("(p s) c -> p s c", s=4)

        def y_store(s):
            nc.sync.dma_start(out=out_v[:, s, :], in_=y_sb[:, s, :])

        def y_store_half(s, c):
            cols = slice(512 * c, 512 * c + 512)
            nc.sync.dma_start(out=out_v[:, s, cols], in_=y_sb[:, s, cols])

        y_grp = [None] * 4
        y_codes = keep.tile([P, C], U32, name="y_codes", align_bytes=64)
        y_scales = keep.tile([P, C], U8, name="y_scales", align_bytes=64)

        def y_mix(c, engine):
            src = y_sb[:, :, 256 * c : 256 * c + 256].rearrange("p s c -> p c s")
            copy(engine, y_grp[c][:], src)

        def y_quant(c):
            cols = slice(256 * c, 256 * c + 256)
            quant(y_grp[c][:].rearrange("p c s -> p (c s)"), y_codes[:, cols], y_scales[:, cols])

        words_v = out_1[0].rearrange("p m s -> p (m s)").bitcast(I32)

        def words_store(c):
            cols = slice(512 * c, 512 * c + 512)
            nc.sync.dma_start(out=words_v[:, cols], in_=y_codes[:, cols].bitcast(I32))

        def words_store4(c):
            cols = slice(256 * c, 256 * c + 256)
            nc.sync.dma_start(out=words_v[:, cols], in_=y_codes[:, cols].bitcast(I32))

        def scales_store():
            dst = out_2[0].bitcast(I32)
            for k in range(4):
                eng = nc.scalar
                eng.dma_start(out=dst[4 * k : 4 * k + 4, :], in_=y_scales[32 * k : 32 * k + 4, :].bitcast(I32))

        for h in range(len(BLOCKS)):
            t_grp[h] = keep.tile([P, 2 * width(h) * 4], BF16, name="t_grp%d" % h, align_bytes=64)
            e_codes[h] = keep.tile([P, 2, width(h)], U32, name="e_codes%d" % h, align_bytes=64)
            e_scales[h] = keep.tile([P, 2, width(h)], U8, name="e_scales%d" % h, align_bytes=64)
            for g in range(2):
                d_sb[(h, g)] = keep.tile([P, 4, width(h)], F32, name="d_sb%d_%d" % (h, g), align_bytes=64)
                z_sb[(h, g)] = keep.tile([P, 4, width(h)], F32, name="z_sb%d_%d" % (h, g), align_bytes=64)
                e_grp[(h, g)] = keep.tile([P, width(h) * 4], BF16, name="e_grp%d_%d" % (h, g), align_bytes=64)
        for a in range(4):
            i1_codes[a] = keep.tile([P, 2, 2, P], U32, name="i1_codes%d" % a, align_bytes=64)
            i1_scales[a] = keep.tile([P, 2, 2, P], U8, name="i1_scales%d" % a, align_bytes=64)
            i1_grp[a] = keep.tile([P, 2 * 1024], BF16, name="i1_grp%d" % a, align_bytes=64)
            i2_grp[a] = keep.tile([P, 512, 4], BF16, name="i2_grp%d" % a, align_bytes=64)
            y_grp[a] = keep.tile([P, 256, 4], BF16, name="y_grp%d" % a, align_bytes=64)

        load_t(1)
        load_t(0)
        load_i1(0)
        dummy(4)
        load_rq()
        load_i1(1)
        load_i2(3)
        load_i1(2)
        load_i2(2)
        load_i1(3)
        load_i2(0)
        load_t2(2)
        load_i2(1)
        dummy(1)
        dummy(1)
        turn_t(1)
        turn_t(0)
        evac_t1(1, "V")
        dummy(1)
        dummy(1)
        evac_t1(0, "A")
        turn_i1s(0)
        quant_t(0)
        turn_i1s(1)
        evac_i1s(0, "A")
        consts_t()
        dummy(1)
        evac_i1s(1, "V")
        dummy(1)
        turn_i1s(2)
        quant_i1(0)
        mix_i2h(3, 0, "A")
        turn_i1s(3)
        mix_i2h(3, 1, "V")
        mx_mean(0, 0)
        mx_mean(0, 1)
        consts_a("A")
        evac_i1s(2, "V")
        turn_i1s(5)
        evac_i1s(3, "A")
        quant_i2(3)
        turn_i1s(4)
        mix_i2h(2, 0, "A")
        quant_i1(1)
        mx_s(0, 0)
        evac_i1s(5, "V")
        mx_s(0, 1)
        mx_mean(0, 2)
        mix_i2h(2, 1, "V")
        turn_i1s(7)
        evac_i1s(4, "A")
        turn_i1s(6)
        quant_i1(2)
        evac_i1s(7, "A")
        mx_mean(0, 3)
        mix_i2h(0, 0, "V")
        consts_mm()
        evac_i1s(6, "A")
        mx_mean(0, 4)
        quant_i2(2)
        mx_mean(0, 5)
        mix_i2h(0, 1, "A")
        turn_t(3)
        quant_i1(3)
        turn_t(2)
        consts_b()
        evac_t1(3, "A")
        mx_mean(0, 6)
        mx_mean(0, 7)
        evac_t1(2, "A")
        mx_s(0, 2)
        quant_i2(0)
        mx_s(0, 3)
        part_sum(0, "A")
        mx_s(0, 5)
        quant_t(1)
        e_x(0, 0, "A")
        mx_s(0, 6)
        sum_mm(0)
        mix_i2h(1, 0, "V")
        mx_s(0, 4)
        mx_mean(1, 0)
        mix_i2h(1, 1, "V")
        sum_out(0, "A")
        mx_mean(1, 1)
        mx_mean(1, 2)
        e_z(0, 1, "A")
        e_z(0, 0, "V")
        mx_mean(1, 3)
        mx_mean(1, 4)
        mx_mean(1, 5)
        mx_mean(1, 6)
        e_t3(0, 0)
        mx_mean(1, 7)
        mx_s(0, 7)
        e_x(0, 1, "A")
        mx_s(1, 6)
        mx_s(1, 5)
        part_sum(1, "V")
        mx_s(1, 4)
        quant_e(0, 0)
        sum_mm(1)
        quant_i2(1)
        mx_s(1, 0)
        e_t3(0, 1)
        mx_s(1, 3)
        sum_out(1, "A")
        mx_s(1, 1)
        mx_s(1, 7)
        e_x(1, 1, "A")
        mx_s(1, 2)
        e_u1(1, 0)
        e_z(1, 1, "A")
        quant_e(0, 1)
        mx_y(0, 0, 1)
        e_u2(1, 0)
        mx_y(0, 0, 0)
        y_evac(0, 0, 1, "A")
        mx_y(0, 1, 1)
        e_t3s(1, 1, 0)
        y_store_half(0, 1)
        quant_e(1, 0)
        mx_y(0, 1, 0)
        y_evac(0, 1, 1, "A")
        e_t3s(1, 1, 1)
        mx_yg(1, 1, 0, 0)
        mx_yg(1, 0, 0, 0)
        quant_es(1, 1, 0)
        y_evac(0, 1, 0, "A")
        y_store_half(1, 1)
        quant_es(1, 1, 1)
        y_evac(0, 0, 0, "V")
        mx_yg(1, 0, 0, 1)
        mx_yg(1, 1, 0, 1)
        y_store_half(1, 0)
        mx_yg(1, 0, 1, 0)
        y_evac(1, 0, 0, "V")
        y_store_half(0, 0)
        mx_yg(1, 0, 1, 1)
        y_evac(1, 1, 0, "A")
        mx_yg(1, 1, 1, 0)
        mx_yg(1, 1, 1, 1)
        y_store_half(2, 0)
        y_evac(1, 0, 1, "A")
        y_store_half(3, 0)
        y_mix(0, "V")
        y_evac(1, 1, 1, "A")
        y_mix(1, "V")
        y_mix(3, "A")
        y_store_half(3, 1)
        y_quant(0)
        y_mix(2, "V")
        words_store4(0)
        y_store_half(2, 1)
        y_quant(1)
        y_quant(2)
        y_quant(3)
        words_store4(2)
        words_store4(1)
        words_store4(3)
        scales_store()
